import numpy as np
import ml_dtypes


def mxq(x, axis, fmt="e4m3"):
    dtype, down = {"e4m3": (ml_dtypes.float8_e4m3fn, 7), "e5m2": (ml_dtypes.float8_e5m2, 14)}[fmt]
    v = np.moveaxis(np.asarray(x, np.float32).astype(ml_dtypes.bfloat16).astype(np.float64), axis, -1)
    blocks = v.reshape(v.shape[:-1] + (-1, 32))
    amax = np.abs(blocks).max(-1, keepdims=True)
    byte = np.maximum(np.where(amax > 0, np.frexp(amax)[1] - 1 + 127, 0) - down, 1)
    scale = np.exp2(byte - 127.0)
    codes = (blocks / scale).astype(np.float32).astype(dtype).astype(np.float64)
    return np.moveaxis((codes * scale).reshape(v.shape), -1, axis)


WIDE = False


def mx_kscale(k):
    if not WIDE:
        return np.ones(k)
    levels = np.array([10, -10, 5, -5, 0])
    if k % 512:
        return np.exp2(np.random.permutation(np.resize(levels, k // 32))).repeat(32)
    a = np.empty((k // 512, 16))
    for p in range(k // 512):
        a[p, :8] = np.random.permutation(np.resize(levels, 8))
        for g in range(8):
            far = levels[np.abs(levels - a[p, g]) >= 10]
            a[p, g + 8] = far[np.random.randint(len(far))]
    return np.exp2(a.ravel()).repeat(32)


BF16 = ml_dtypes.bfloat16


def bf(x):
    return np.asarray(x, np.float32).astype(BF16)


def f64(x):
    return np.asarray(x).astype(np.float64)


E2M1 = np.array([0.0, 0.5, 1.0, 1.5, 2.0, 3.0, 4.0, 6.0, -0.0, -0.5, -1.0, -1.5, -2.0, -3.0, -4.0, -6.0])


def pack_weight(w, fmt):
    k, n = w.shape
    w = f64(bf(w)).reshape(k // 32, 32, n)
    amax = np.abs(w).max(1)
    if fmt == "e4m3":
        byte = np.frexp(amax)[1] - 1 + 127 - 7
    else:
        mant, ex = np.frexp(amax / 6.0)
        byte = np.where(mant > 0.5, ex, ex - 1) + 127
    byte = np.clip(np.where(amax > 0, byte, 1), 1, 254)
    scaled = (w * np.exp2(127.0 - byte)[:, None, :]).reshape(k, n).astype(np.float32)
    by_word = np.ascontiguousarray(scaled.reshape(k // 512, 128, 4, n).transpose(0, 1, 3, 2))
    if fmt == "e4m3":
        words = by_word.astype(ml_dtypes.float8_e4m3fn).view(np.uint8)
    else:
        c = by_word.astype(ml_dtypes.float4_e2m1fn).view(np.uint8) & 0xF
        words = c[..., 0::2] | (c[..., 1::2] << 4)
    return np.ascontiguousarray(words), np.ascontiguousarray(byte.astype(np.uint8).reshape(k // 512, 16, n))


def unpack_weight(words, scales, fmt):
    g, p, n, _ = words.shape
    if fmt == "e4m3":
        vals = np.ascontiguousarray(words).view(ml_dtypes.float8_e4m3fn).astype(np.float64)
    else:
        nib = np.empty((g, p, n, 4), np.uint8)
        nib[..., 0::2] = words & 0xF
        nib[..., 1::2] = words >> 4
        vals = E2M1[nib]
    vals = vals * np.repeat(np.exp2(scales.astype(np.float64) - 127.0), 8, axis=1)[..., None]
    return vals.transpose(0, 1, 3, 2).reshape(g * 512, n)
def pack4(w):
    words, scales = pack_weight(w, "e2m1")
    return words.reshape(words.shape[0], 128, -1), scales


def unpack4(words, scales):
    return unpack_weight(words.reshape(words.shape[0], 128, -1, 2), scales, "e2m1")


E4M3FN = np.array([(-1.0 if i & 128 else 1.0) * ((1.0 + (i & 7) / 8.0) * 2.0 ** (((i >> 3) & 15) - 7) if i & 120 else (i & 7) * 2.0 ** -9) for i in range(256)])


def e4m3fn_bytes(y):
    return np.clip(np.asarray(y, np.float64), -448.0, 448.0).astype(np.float32).astype(ml_dtypes.float8_e4m3fn).view(np.uint8)


def e4m3fn_values(b):
    return E4M3FN[b]


N, D, F = 512, 1024, 2048


def draw0():
    s, t = mx_kscale(D), mx_kscale(F)
    x = bf(np.random.standard_normal((N, D)) * s)
    w_gate_words, w_gate_scales = pack4(np.random.standard_normal((D, F)) / np.sqrt(D) / s[:, None])
    b_gate = bf(0.3 * np.random.standard_normal(F))
    r_mag = bf(0.3 * np.random.standard_normal(F))
    b_mag = bf(0.3 * np.random.standard_normal(F))
    g_feat = bf(np.random.standard_normal(F) * t)
    w_dec_words, w_dec_scales = pack4(np.random.standard_normal((F, D)) / np.sqrt(F) / t[:, None])
    return {
        "x": x,
        "w_gate_words": w_gate_words,
        "w_gate_scales": w_gate_scales,
        "b_gate": b_gate,
        "r_mag": r_mag,
        "b_mag": b_mag,
        "g_feat": g_feat,
        "w_dec_words": w_dec_words,
        "w_dec_scales": w_dec_scales,
    }


def core(x, w_gate_words, w_gate_scales, b_gate, r_mag, b_mag, g_feat, w_dec_words, w_dec_scales):
    u = mxq(f64(x), 1, "e4m3") @ unpack4(w_gate_words, w_gate_scales)
    pg = u + f64(b_gate)[None, :]
    pm = np.exp(f64(r_mag))[None, :] * u + f64(b_mag)[None, :]
    f = np.where(pg > 0.0, np.maximum(pm, 0.0), 0.0)
    g = f64(g_feat)[None, :]
    f_scaled = f * g
    a_scaled = np.maximum(pg, 0.0) * g
    wq = unpack4(w_dec_words, w_dec_scales)
    xhat = mxq(f_scaled, 1, "e4m3") @ wq
    xaux = mxq(a_scaled, 1, "e4m3") @ wq
    return xhat, xaux


def setup_inputs():
    drawn = draw0()
    full = np.asarray(drawn['x']).astype(np.float64)
    scale = (np.abs(full).reshape(512, 8, 128).max(axis=(2,)) / 448.0).astype(np.float32)
    given = {}
    for key, value in drawn.items():
        if key == 'x':
            given['x_bytes'] = e4m3fn_bytes(full / np.repeat(scale.astype(np.float64), 128, axis=1))
            given['x_scale'] = scale
        else:
            given[key] = value
    return given


def reference(x_bytes, x_scale, w_gate_words, w_gate_scales, b_gate, r_mag, b_mag, g_feat, w_dec_words, w_dec_scales):
    return core(e4m3fn_values(x_bytes) * np.repeat(x_scale.astype(np.float64), 128, axis=1), w_gate_words, w_gate_scales, b_gate, r_mag, b_mag, g_feat, w_dec_words, w_dec_scales)

@@ -1,0 +1,319 @@
+from contextlib import ExitStack
+
+import concourse.mybir as mybir
+from concourse.masks import make_identity
+
+N, D, F = 512, 1024, 2048
+FLOPS = 2 * N * D * F * 3
+
+F32 = mybir.dt.float32
+BF16 = mybir.dt.bfloat16
+I32 = mybir.dt.int32
+U32 = mybir.dt.uint32
+U8 = mybir.dt.uint8
+FP8 = mybir.dt.float8_e4m3fn
+FP8X4 = mybir.dt.float8_e4m3fn_x4
+FP4X4 = mybir.dt.float4_e2m1fn_x4
+ACT = mybir.ActivationFunctionType
+ALU = mybir.AluOpType
+
+P = 128
+PACK = 4
+TILES = N // P
+XPASS = D // 512
+GROUPS = F // 512
+HALVES = D // 512
+XBLOCKS = D // 128
+VEC_BLOCKS = 4
+U_BANKS = (6, 7)
+WARM = 5
+
+
+def tile_gatedsparseautoencoderwithaux_d1p_kernel(
+    tc, x_bytes, x_scale, w_gate_words, w_gate_scales, b_gate, r_mag, b_mag, g_feat,
+    w_dec_words, w_dec_scales, out_0, out_1,
+):
+    nc = tc.nc
+    with ExitStack() as ctx:
+        sb = ctx.enter_context(tc.tile_pool(name="sb", bufs=1))
+        psum = ctx.enter_context(tc.psum_pool(name="psum", bufs=1))
+        ctx.enter_context(tc.manual_schedule())
+
+        def tile(shape, dtype, name):
+            return sb.tile(shape, dtype, name=name, align_bytes=64)
+
+        bank = [psum.tile([P, 512], F32, name="bank%d" % i) for i in range(8)]
+
+        xs = tile([P, TILES, XBLOCKS], F32, "xs")
+        xb = [tile([P, 2, D], U8, "xbytes%d" % i) for i in range(2)]
+        xw = [tile([P, D], BF16, "xw%d" % j) for j in range(TILES)]
+        xg = [tile([P, XPASS, P, PACK], BF16, "xg%d" % j) for j in range(TILES)]
+        xq = [tile([P, N], U32, "xq%d" % g) for g in range(XPASS)]
+        xqs = [tile([P, N], U8, "xqs%d" % g) for g in range(XPASS)]
+        ident = tile([P, P], F32, "ident")
+
+        gs_raw = [tile([P, XPASS, F // 2], U8, "gs_raw%d" % i) for i in range(2)]
+        zeros = tile([P, 512], BF16, "zeros")
+        gw_raw = [tile([P, XPASS, 1024], U8, "gw_raw%d" % G) for G in range(GROUPS)]
+        gw = [tile([P, PACK, XPASS, 256], U8, "gw%d" % G) for G in range(GROUPS)]
+        gs = [tile([P, PACK, XPASS, P], U8, "gs%d" % G) for G in range(GROUPS)]
+        dw = [tile([P, 2 * D], U8, "dw%d" % G) for G in range(GROUPS)]
+        ds = tile([P, GROUPS, D], U8, "ds")
+
+        vb = tile([P, GROUPS, PACK], BF16, "vb")
+        vr = tile([P, GROUPS, PACK], BF16, "vr")
+        vm = tile([P, GROUPS, PACK], BF16, "vm")
+        vg = tile([P, GROUPS, PACK], BF16, "vg")
+        warm_out = tile([P, 1], F32, "warm_out")
+        er = tile([P, GROUPS, PACK], F32, "er")
+        ag = tile([P, GROUPS, PACK], F32, "ag")
+        sg = tile([P, GROUPS, PACK], F32, "sg")
+        a_bias = tile([P, GROUPS, PACK], F32, "a_bias")
+        m_scale = tile([P, GROUPS, PACK], F32, "m_scale")
+        m_bias = tile([P, GROUPS, PACK], F32, "m_bias")
+
+        a_abs = [[tile([P, N], BF16, "a_abs%d_%d" % (G, t)) for t in range(PACK)] for G in range(GROUPS)]
+        m_abs = [tile([P, PACK, 2, N], BF16, "m_abs%d" % gh) for gh in range(2)]
+        gate = [tile([P, PACK, 2, N], BF16, "gate%d" % gh) for gh in range(2)]
+        a_pl = [tile([P, PACK, N], BF16, "a_pl%d" % G) for G in range(GROUPS)]
+        a_il = [tile([P, N, PACK], BF16, "a_il%d" % G) for G in range(GROUPS)]
+        aq = [tile([P, N], U32, "aq%d" % G) for G in range(GROUPS)]
+        aqs = [tile([P, N], U8, "aqs%d" % G) for G in range(GROUPS)]
+        f_pl = [[tile([P, PACK, 2, P], BF16, "f_pl%d_%d" % (j, gh)) for gh in range(2)] for j in range(TILES)]
+        f_il = [[tile([P, 2 * P, PACK], BF16, "f_il%d_%d" % (j, gh)) for gh in range(2)] for j in range(TILES)]
+        fq = [[tile([P, 2 * P], U32, "fq%d_%d" % (j, gh)) for gh in range(2)] for j in range(TILES)]
+        fqs = [[tile([P, 2 * P], U8, "fqs%d_%d" % (j, gh)) for gh in range(2)] for j in range(TILES)]
+        res = [[[tile([P, 512], F32, "res%d_%d_%d" % (o, j, h)) for h in range(HALVES)] for j in range(TILES)] for o in range(2)]
+
+        nc.vector.memset(gs_raw[0][:].rearrange("p g n -> p (g n)").bitcast(I32), 0)
+        nc.vector.memset(zeros[:], 0.0)
+        nc.vector.memset(gs_raw[1][:].rearrange("p g n -> p (g n)").bitcast(I32), 0)
+        nc.vector.memset(ds[:].rearrange("p g n -> p (g n)").bitcast(I32), 0)
+        make_identity(nc, ident[:])
+        nc.scalar.activation(out=warm_out[:], in_=zeros[:, 0:1], func=ACT.Exp)
+        for i in range(WARM):
+            nc.tensor.matmul(bank[7][:], lhsT=zeros[:, 0:P], rhs=zeros[:], start=True, stop=True)
+
+        def load_gate_scales(i):
+            for Q in range(4):
+                nc.sync.dma_start(
+                    out=gs_raw[i][32 * Q : 32 * Q + 4].bitcast(I32),
+                    in_=w_gate_scales[:, 4 * Q : 4 * Q + 4, 1024 * i : 1024 * (i + 1)].rearrange("g r n -> r g n").bitcast(I32),
+                )
+
+        gate_rows = w_gate_words.rearrange("g p n -> p g n")
+
+        def load_gate_words(G):
+            nc.sync.dma_start(out=gw_raw[G][:].bitcast(I32), in_=gate_rows[:, :, 1024 * G : 1024 * (G + 1)].bitcast(I32))
+
+        x_rows = x_bytes.rearrange("(p j) k -> p j k", j=TILES)
+        nc.sync.dma_start(out=xs[:], in_=x_scale.rearrange("(p j) b -> p j b", j=TILES))
+        for i in range(2):
+            nc.sync.dma_start(out=xb[i][:], in_=x_rows[:, 2 * i : 2 * i + 2, :])
+        load_gate_words(0)
+        load_gate_scales(0)
+        for v_tile, v in ((vg, g_feat), (vr, r_mag), (vb, b_gate), (vm, b_mag)):
+            nc.sync.dma_start(out=v_tile[:], in_=v.rearrange("(g p t) -> p g t", p=P, t=PACK))
+        load_gate_words(1)
+        load_gate_scales(1)
+        load_gate_words(2)
+        load_gate_words(3)
+        for Q in range(4):
+            nc.sync.dma_start(
+                out=ds[32 * Q : 32 * Q + 4].bitcast(I32),
+                in_=w_dec_scales[:, 4 * Q : 4 * Q + 4, :].rearrange("g r n -> r g n").bitcast(I32),
+            )
+        for G in range(GROUPS):
+            nc.sync.dma_start(out=dw[G][:].bitcast(I32), in_=w_dec_words[G].bitcast(I32))
+
+        def widen(j):
+            src = xb[j // 2][:, j % 2, :].bitcast(FP8)
+            for b in range(XBLOCKS):
+                cols = slice(128 * b, 128 * (b + 1))
+                if b < VEC_BLOCKS:
+                    nc.vector.tensor_scalar(out=xw[j][:, cols], in0=src[:, cols], scalar1=xs[:, j, b : b + 1], scalar2=None, op0=ALU.mult)
+                else:
+                    nc.scalar.activation(out=xw[j][:, cols], in_=src[:, cols], func=ACT.Copy, scale=xs[:, j, b : b + 1])
+
+        def turn(j):
+            words = xw[j][:].bitcast(F32)
+            for g in range(XPASS):
+                for u in range(2):
+                    c = 128 * (2 * g + u)
+                    nc.tensor.transpose(bank[j][:, c : c + 128], words[:, 256 * g + u : 256 * (g + 1) : 2], ident[:])
+
+        def turn_out(j):
+            nc.scalar.copy(
+                out=xg[j][:].bitcast(F32),
+                in_=bank[j][:].rearrange("p (g u r) -> p g r u", g=XPASS, u=2),
+            )
+
+        def quantize(codes, scales, src):
+            nc.vector.quantize_mx(out=codes.bitcast(FP8X4), scales=scales, in_=src)
+
+        def quant_x(j):
+            for g in range(XPASS):
+                cols = slice(128 * j, 128 * (j + 1))
+                quantize(xq[g][:, cols], xqs[g][:, cols], xg[j][:, g].rearrange("p r t -> p (r t)"))
+
+        def perm_words(G):
+            nc.vector.tensor_copy(
+                out=gw[G][:].rearrange("p t g n -> p t (g n)").rearrange("p t (c b) -> p t c b", b=2),
+                in_=gw_raw[G][:].rearrange("p g n -> p (g n)").rearrange("p (c t b) -> p t c b", t=PACK, b=2),
+            )
+
+        def perm_scales(G):
+            nc.vector.tensor_copy(
+                out=gs[G][:],
+                in_=gs_raw[G // 2][:, :, 512 * (G % 2) : 512 * (G % 2 + 1)].rearrange("p g (m t) -> p t g m", t=PACK),
+            )
+
+        def encode(G, t):
+            u = bank[U_BANKS[t % 2]]
+            for g in range(XPASS):
+                nc.tensor.matmul_mx(
+                    out=u[:], lhsT=gw[G][:, t, g, :].bitcast(FP4X4), lhsT_scale=gs[G][:, t, g, :],
+                    rhs=xq[g][:].bitcast(FP8X4), rhs_scale=xqs[g][:], start=(g == 0), stop=(g == XPASS - 1),
+                )
+
+        def activate(G, t):
+            u = bank[U_BANKS[t % 2]]
+            nc.scalar.activation(out=a_abs[G][t][:], in_=u[:], func=ACT.Relu, scale=ag[:, G, t : t + 1], bias=a_bias[:, G, t : t + 1])
+            nc.scalar.activation(out=m_abs[G // 2][:, t, G % 2, :], in_=u[:], func=ACT.Relu, scale=m_scale[:, G, t : t + 1], bias=m_bias[:, G, t : t + 1])
+
+        def signs(G, t):
+            nc.vector.tensor_scalar(out=a_pl[G][:, t, :], in0=a_abs[G][t][:], scalar1=sg[:, G, t : t + 1], scalar2=None, op0=ALU.mult)
+            nc.vector.tensor_scalar(out=gate[G // 2][:, t, G % 2, :], in0=a_abs[G][t][:], scalar1=0.0, scalar2=sg[:, G, t : t + 1], op0=ALU.is_gt, op1=ALU.mult)
+
+        def interleave(dst, src, on_scalar=False):
+            out = dst.rearrange("p (c i) t -> p c t i", i=4)
+            in_ = src.rearrange("p t (c i) -> p c t i", i=4)
+            if on_scalar:
+                nc.scalar.copy(out=out, in_=in_)
+            else:
+                nc.vector.tensor_copy(out=out, in_=in_)
+
+        def il_a(G, n0=0, n1=N):
+            interleave(a_il[G][:, n0:n1, :], a_pl[G][:, :, n0:n1])
+
+        def quant_a(G, n0=0, n1=N):
+            quantize(aq[G][:, n0:n1], aqs[G][:, n0:n1], a_il[G][:, n0:n1, :].rearrange("p n t -> p (n t)"))
+
+        def gate_f(j, gh):
+            cols = slice(P * j, P * (j + 1))
+            nc.vector.tensor_tensor(out=f_pl[j][gh][:], in0=gate[gh][:, :, :, cols], in1=m_abs[gh][:, :, :, cols], op=ALU.mult)
+
+        def il_f(j, gh, on_scalar=False):
+            interleave(f_il[j][gh][:], f_pl[j][gh][:].rearrange("p t g r -> p t (g r)"), on_scalar)
+
+        def quant_f(j, gh):
+            quantize(fq[j][gh][:], fqs[j][gh][:], f_il[j][gh][:].rearrange("p n t -> p (n t)"))
+
+        def decode(o, j, h, G):
+            if o == 1:
+                codes, scales = aq[G][:, P * j : P * (j + 1)], aqs[G][:, P * j : P * (j + 1)]
+            else:
+                c = P * (G % 2)
+                codes, scales = fq[j][G // 2][:, c : c + P], fqs[j][G // 2][:, c : c + P]
+            nc.tensor.matmul_mx(
+                out=bank[2 * j + h][:], lhsT=codes.bitcast(FP8X4), lhsT_scale=scales,
+                rhs=dw[G][:, 1024 * h : 1024 * (h + 1)].bitcast(FP4X4), rhs_scale=ds[:, G, 512 * h : 512 * (h + 1)],
+                start=(G == 0), stop=(G == GROUPS - 1),
+            )
+
+        outs = [o.rearrange("(p j) d -> j p d", j=TILES) for o in (out_0, out_1)]
+
+        def finish(o, j, h, on_vector=False):
+            if on_vector:
+                nc.vector.tensor_copy(out=res[o][j][h][:], in_=bank[2 * j + h][:])
+            else:
+                nc.scalar.copy(out=res[o][j][h][:], in_=bank[2 * j + h][:])
+            nc.sync.dma_start(out=outs[o][j][:, 512 * h : 512 * (h + 1)], in_=res[o][j][h][:])
+
+        def keep_warm():
+            nc.tensor.matmul(bank[7][:], lhsT=zeros[:, 0:P], rhs=zeros[:], start=True, stop=True)
+
+        widen(0)
+        turn(0)
+        widen(1)
+        turn(1)
+        keep_warm()
+        widen(2)
+        turn(2)
+        turn_out(0)
+        widen(3)
+        turn(3)
+        keep_warm()
+        turn_out(1)
+        turn_out(2)
+        turn_out(3)
+        nc.scalar.activation(out=er[:], in_=vr[:], func=ACT.Exp)
+        nc.scalar.activation(out=ag[:], in_=vg[:], func=ACT.Abs)
+        nc.scalar.activation(out=sg[:], in_=vg[:], func=ACT.Sign)
+        perm_words(0)
+        quant_x(0)
+        perm_scales(0)
+        quant_x(1)
+        quant_x(2)
+        quant_x(3)
+        nc.vector.tensor_tensor(out=a_bias[:], in0=ag[:], in1=vb[:], op=ALU.mult)
+        nc.vector.tensor_tensor(out=m_scale[:], in0=ag[:], in1=er[:], op=ALU.mult)
+        nc.vector.tensor_tensor(out=m_bias[:], in0=ag[:], in1=vm[:], op=ALU.mult)
+        perm_words(1)
+        perm_scales(1)
+
+        fill = {
+            (0, 1): [lambda: perm_words(2)], (0, 2): [lambda: perm_scales(2)], (0, 3): [lambda: perm_scales(3)],
+            (1, 2): [lambda: perm_words(3)],
+            (2, 2): [lambda: gate_f(0, 0)], (2, 3): [lambda: gate_f(1, 0)],
+            (3, 2): [lambda: gate_f(2, 0)], (3, 3): [lambda: gate_f(3, 0)],
+        }
+        early = [(j, h) for j in range(TILES - 1) for h in range(HALVES)]
+        last = TILES - 1
+        encode(0, 0)
+        encode(0, 1)
+        for G in range(GROUPS):
+            for t in range(PACK):
+                activate(G, t)
+                for work in fill.get((G, t), []):
+                    work()
+                signs(G, t)
+                if t == 0 and G > 0:
+                    quant_a(G - 1)
+                if t == PACK - 1 and G < GROUPS - 1:
+                    il_a(G)
+                s = PACK * G + t + 2
+                if s < PACK * GROUPS:
+                    encode(s // PACK, s % PACK)
+                if G > 0 and t > 0:
+                    for j, h in early[2 * (t - 1) : 2 * t]:
+                        decode(1, j, h, G - 1)
+
+        G = GROUPS - 1
+        for h in range(HALVES):
+            for g in range(GROUPS - 1):
+                decode(1, last, h, g)
+        il_f(0, 0, on_scalar=True)
+        il_a(G, 0, N // 2)
+        il_a(G, N // 2, N)
+        quant_a(G, 0, N // 2)
+        gate_f(0, 1)
+        quant_a(G, N // 2, N)
+        for j in range(TILES):
+            for h in range(HALVES):
+                decode(1, j, h, G)
+                finish(1, j, h)
+        il_f(0, 1)
+        quant_f(0, 0)
+        for j in range(TILES):
+            if j < last:
+                il_f(j + 1, 0)
+            quant_f(j, 1)
+            if j < last:
+                gate_f(j + 1, 1)
+                quant_f(j + 1, 0)
+                il_f(j + 1, 1)
+            for h in range(HALVES):
+                for g in range(GROUPS):
+                    decode(0, j, h, g)
+                finish(0, j, h, on_vector=(j == last and h == 1))

@@ -4,7 +4,7 @@ import concourse.mybir as mybir
 from concourse.masks import make_identity
 
 N, D, F = 512, 1024, 2048
-FLOPS = 2 * N * D * F * 3
+FLOPS = 3 * 2 * N * D * F
 
 F32 = mybir.dt.float32
 BF16 = mybir.dt.bfloat16
@@ -19,14 +19,24 @@ ALU = mybir.AluOpType
 
 P = 128
 PACK = 4
+K_PASS = P * PACK
+BANK = 512
+FP4_WORD = 2
+QUADRANTS = 4
 TILES = N // P
-XPASS = D // 512
-GROUPS = F // 512
-HALVES = D // 512
-XBLOCKS = D // 128
-VEC_BLOCKS = 4
-U_BANKS = (6, 7)
-WARM = 5
+X_PASSES = D // K_PASS
+GROUPS = F // K_PASS
+PAIRS = GROUPS // 2
+HALVES = D // BANK
+X_BLOCK = 128
+X_BLOCKS = D // X_BLOCK
+X_LOADS = ((0, 1), (1, 1), (2, 2))
+XHAT, XAUX = 0, 1
+LAST = TILES - 1
+
+U_BANKS = (2 * LAST, 2 * LAST + 1)
+VECTOR_BANK = TILES
+WARMUP_MATMULS = (9, 2, 3)
 
 
 def tile_gatedsparseautoencoderwithaux_d1p_kernel(
@@ -35,285 +45,334 @@ def tile_gatedsparseautoencoderwithaux_d1p_kernel(
 ):
     nc = tc.nc
     with ExitStack() as ctx:
-        sb = ctx.enter_context(tc.tile_pool(name="sb", bufs=1))
+        sbuf = ctx.enter_context(tc.tile_pool(name="sbuf", bufs=1))
         psum = ctx.enter_context(tc.psum_pool(name="psum", bufs=1))
         ctx.enter_context(tc.manual_schedule())
 
         def tile(shape, dtype, name):
-            return sb.tile(shape, dtype, name=name, align_bytes=64)
+            return sbuf.tile(shape, dtype, name=name, align_bytes=64)
 
-        bank = [psum.tile([P, 512], F32, name="bank%d" % i) for i in range(8)]
+        bank = [psum.tile([P, BANK], F32, name="bank%d" % i) for i in range(TILES * HALVES)]
 
-        xs = tile([P, TILES, XBLOCKS], F32, "xs")
-        xb = [tile([P, 2, D], U8, "xbytes%d" % i) for i in range(2)]
-        xw = [tile([P, D], BF16, "xw%d" % j) for j in range(TILES)]
-        xg = [tile([P, XPASS, P, PACK], BF16, "xg%d" % j) for j in range(TILES)]
-        xq = [tile([P, N], U32, "xq%d" % g) for g in range(XPASS)]
-        xqs = [tile([P, N], U8, "xqs%d" % g) for g in range(XPASS)]
+        xs = tile([P, TILES, X_BLOCKS], F32, "xs")
+        xb = [tile([P, n, D], U8, "xbytes%d" % i) for i, (j0, n) in enumerate(X_LOADS)]
+        x_rows = [tile([P, D], BF16, "x_rows%d" % j) for j in range(TILES)]
+        x_turned = [tile([P, X_PASSES, P, PACK], BF16, "x_turned%d" % j) for j in range(TILES)]
+        x_codes = [tile([P, N], U32, "x_codes%d" % g) for g in range(X_PASSES)]
+        x_scales = [tile([P, N], U8, "x_scales%d" % g) for g in range(X_PASSES)]
         ident = tile([P, P], F32, "ident")
 
-        gs_raw = [tile([P, XPASS, F // 2], U8, "gs_raw%d" % i) for i in range(2)]
-        zeros = tile([P, 512], BF16, "zeros")
-        gw_raw = [tile([P, XPASS, 1024], U8, "gw_raw%d" % G) for G in range(GROUPS)]
-        gw = [tile([P, PACK, XPASS, 256], U8, "gw%d" % G) for G in range(GROUPS)]
-        gs = [tile([P, PACK, XPASS, P], U8, "gs%d" % G) for G in range(GROUPS)]
-        dw = [tile([P, 2 * D], U8, "dw%d" % G) for G in range(GROUPS)]
+        gs_first_raw = tile([P, X_PASSES, K_PASS], U8, "gs_first_raw")
+        gs_rest_raw = tile([P, F - K_PASS], U8, "gs_rest_raw")
+        zeros = tile([P, BANK], BF16, "zeros")
+        gw_raw = [tile([P, X_PASSES, K_PASS * FP4_WORD], U8, "gw_raw%d" % G) for G in range(GROUPS)]
+        gw = [tile([P, PACK, X_PASSES, P * FP4_WORD], U8, "gw%d" % G) for G in range(GROUPS)]
+        gs_first = tile([P, X_PASSES, PACK, P], U8, "gs_first")
+        gs_rest = [tile([P, GROUPS - 1, PACK, P], U8, "gs_rest%d" % g) for g in range(X_PASSES)]
+        dw = [tile([P, D * FP4_WORD], U8, "dw%d" % G) for G in range(GROUPS)]
         ds = tile([P, GROUPS, D], U8, "ds")
 
-        vb = tile([P, GROUPS, PACK], BF16, "vb")
-        vr = tile([P, GROUPS, PACK], BF16, "vr")
-        vm = tile([P, GROUPS, PACK], BF16, "vm")
-        vg = tile([P, GROUPS, PACK], BF16, "vg")
-        warm_out = tile([P, 1], F32, "warm_out")
-        er = tile([P, GROUPS, PACK], F32, "er")
-        ag = tile([P, GROUPS, PACK], F32, "ag")
-        sg = tile([P, GROUPS, PACK], F32, "sg")
+        vectors = (g_feat, r_mag, b_gate, b_mag)
+        vec_rows = tile([P, K_PASS], BF16, "vec_rows")
+        vec = tile([P, len(vectors), GROUPS, PACK], BF16, "vec")
+        gain, log_mag, gate_bias, mag_bias = (vec[:, i] for i in range(len(vectors)))
+        table_warmup = tile([P, 1], F32, "table_warmup")
+        exp_mag = tile([P, GROUPS, PACK], F32, "exp_mag")
+        abs_gain = tile([P, GROUPS, PACK], F32, "abs_gain")
+        sign_gain = tile([P, GROUPS, PACK], F32, "sign_gain")
         a_bias = tile([P, GROUPS, PACK], F32, "a_bias")
         m_scale = tile([P, GROUPS, PACK], F32, "m_scale")
         m_bias = tile([P, GROUPS, PACK], F32, "m_bias")
 
         a_abs = [[tile([P, N], BF16, "a_abs%d_%d" % (G, t)) for t in range(PACK)] for G in range(GROUPS)]
-        m_abs = [tile([P, PACK, 2, N], BF16, "m_abs%d" % gh) for gh in range(2)]
-        gate = [tile([P, PACK, 2, N], BF16, "gate%d" % gh) for gh in range(2)]
-        a_pl = [tile([P, PACK, N], BF16, "a_pl%d" % G) for G in range(GROUPS)]
-        a_il = [tile([P, N, PACK], BF16, "a_il%d" % G) for G in range(GROUPS)]
-        aq = [tile([P, N], U32, "aq%d" % G) for G in range(GROUPS)]
-        aqs = [tile([P, N], U8, "aqs%d" % G) for G in range(GROUPS)]
-        f_pl = [[tile([P, PACK, 2, P], BF16, "f_pl%d_%d" % (j, gh)) for gh in range(2)] for j in range(TILES)]
-        f_il = [[tile([P, 2 * P, PACK], BF16, "f_il%d_%d" % (j, gh)) for gh in range(2)] for j in range(TILES)]
-        fq = [[tile([P, 2 * P], U32, "fq%d_%d" % (j, gh)) for gh in range(2)] for j in range(TILES)]
-        fqs = [[tile([P, 2 * P], U8, "fqs%d_%d" % (j, gh)) for gh in range(2)] for j in range(TILES)]
-        res = [[[tile([P, 512], F32, "res%d_%d_%d" % (o, j, h)) for h in range(HALVES)] for j in range(TILES)] for o in range(2)]
+        m_abs = [tile([P, PACK, 2, N], BF16, "m_abs%d" % pair) for pair in range(PAIRS)]
+        gate = [tile([P, PACK, 2, N], BF16, "gate%d" % pair) for pair in range(PAIRS)]
+        a_planes = [tile([P, PACK, N], BF16, "a_planes%d" % G) for G in range(GROUPS)]
+        a_packed = [tile([P, N, PACK], BF16, "a_packed%d" % G) for G in range(GROUPS)]
+        a_codes = [tile([P, N], U32, "a_codes%d" % G) for G in range(GROUPS)]
+        a_scales = [tile([P, N], U8, "a_scales%d" % G) for G in range(GROUPS)]
+        f_planes = [tile([P, TILES, PACK, 2, P], BF16, "f_planes%d" % pair) for pair in range(PAIRS)]
+        f_packed = [[tile([P, 2 * P, PACK], BF16, "f_packed%d_%d" % (j, pair)) for pair in range(PAIRS)] for j in range(TILES)]
+        f_codes = [[tile([P, 2 * P], U32, "f_codes%d_%d" % (j, pair)) for pair in range(PAIRS)] for j in range(TILES)]
+        f_scales = [[tile([P, 2 * P], U8, "f_scales%d_%d" % (j, pair)) for pair in range(PAIRS)] for j in range(TILES)]
+        result = [
+            [[tile([P, BANK], F32, "result%d_%d_%d" % (o, j, h)) for h in range(HALVES)] for j in range(TILES)]
+            for o in (XHAT, XAUX)
+        ]
 
-        nc.vector.memset(gs_raw[0][:].rearrange("p g n -> p (g n)").bitcast(I32), 0)
+        nc.vector.memset(gs_first_raw[:].rearrange("p g n -> p (g n)").bitcast(I32), 0)
         nc.vector.memset(zeros[:], 0.0)
-        nc.vector.memset(gs_raw[1][:].rearrange("p g n -> p (g n)").bitcast(I32), 0)
-        nc.vector.memset(ds[:].rearrange("p g n -> p (g n)").bitcast(I32), 0)
+        nc.vector.memset(vec_rows[:], 0.0)
+        nc.vector.memset(gs_rest_raw[:].bitcast(I32), 0)
+        nc.vector.memset(gs_rest[1][:].rearrange("p G t m -> p (G t m)").bitcast(I32), 0)
+        nc.vector.memset(ds[:].rearrange("p G n -> p (G n)").bitcast(I32), 0)
         make_identity(nc, ident[:])
-        nc.scalar.activation(out=warm_out[:], in_=zeros[:, 0:1], func=ACT.Exp)
-        for i in range(WARM):
-            nc.tensor.matmul(bank[7][:], lhsT=zeros[:, 0:P], rhs=zeros[:], start=True, stop=True)
 
-        def load_gate_scales(i):
-            for Q in range(4):
-                nc.sync.dma_start(
-                    out=gs_raw[i][32 * Q : 32 * Q + 4].bitcast(I32),
-                    in_=w_gate_scales[:, 4 * Q : 4 * Q + 4, 1024 * i : 1024 * (i + 1)].rearrange("g r n -> r g n").bitcast(I32),
-                )
+        def warm_up(matmuls):
+            for i in range(matmuls):
+                nc.tensor.matmul(bank[U_BANKS[1]][:], lhsT=zeros[:, 0:P], rhs=zeros[:], start=True, stop=True)
 
-        gate_rows = w_gate_words.rearrange("g p n -> p g n")
+        nc.scalar.activation(out=table_warmup[:], in_=zeros[:, 0:1], func=ACT.Exp)
+        warm_up(WARMUP_MATMULS[0])
+
+        nc.sync.dma_start(out=xs[:], in_=x_scale.rearrange("(r j) b -> r j b", j=TILES))
+        for i, (j0, n) in enumerate(X_LOADS):
+            nc.sync.dma_start(out=xb[i][:], in_=x_bytes.rearrange("(r j) k -> r j k", j=TILES)[:, j0 : j0 + n, :])
 
         def load_gate_words(G):
-            nc.sync.dma_start(out=gw_raw[G][:].bitcast(I32), in_=gate_rows[:, :, 1024 * G : 1024 * (G + 1)].bitcast(I32))
+            cols = slice(K_PASS * FP4_WORD * G, K_PASS * FP4_WORD * (G + 1))
+            nc.sync.dma_start(out=gw_raw[G][:].bitcast(I32), in_=w_gate_words.rearrange("g p n -> p g n")[:, :, cols].bitcast(I32))
 
-        x_rows = x_bytes.rearrange("(p j) k -> p j k", j=TILES)
-        nc.sync.dma_start(out=xs[:], in_=x_scale.rearrange("(p j) b -> p j b", j=TILES))
-        for i in range(2):
-            nc.sync.dma_start(out=xb[i][:], in_=x_rows[:, 2 * i : 2 * i + 2, :])
         load_gate_words(0)
-        load_gate_scales(0)
-        for v_tile, v in ((vg, g_feat), (vr, r_mag), (vb, b_gate), (vm, b_mag)):
-            nc.sync.dma_start(out=v_tile[:], in_=v.rearrange("(g p t) -> p g t", p=P, t=PACK))
-        load_gate_words(1)
-        load_gate_scales(1)
-        load_gate_words(2)
-        load_gate_words(3)
-        for Q in range(4):
+        for i, v in enumerate(vectors):
+            nc.sync.dma_start(out=vec_rows[GROUPS * i : GROUPS * (i + 1), :], in_=v.rearrange("(G n) -> G n", G=GROUPS))
+        for Q in range(QUADRANTS):
             nc.sync.dma_start(
-                out=ds[32 * Q : 32 * Q + 4].bitcast(I32),
-                in_=w_dec_scales[:, 4 * Q : 4 * Q + 4, :].rearrange("g r n -> r g n").bitcast(I32),
+                out=gs_first_raw[32 * Q : 32 * Q + PACK].bitcast(I32),
+                in_=w_gate_scales[:, PACK * Q : PACK * (Q + 1), 0:K_PASS].rearrange("g r n -> r g n").bitcast(I32),
+            )
+        for Q in range(QUADRANTS):
+            nc.sync.dma_start(
+                out=gs_rest_raw[32 * Q : 32 * Q + X_PASSES * PACK].bitcast(I32),
+                in_=w_gate_scales[:, PACK * Q : PACK * (Q + 1), K_PASS:F].bitcast(I32),
+            )
+        for G in range(1, GROUPS):
+            load_gate_words(G)
+        for Q in range(QUADRANTS):
+            nc.sync.dma_start(
+                out=ds[32 * Q : 32 * Q + PACK].bitcast(I32),
+                in_=w_dec_scales[:, PACK * Q : PACK * (Q + 1), :].rearrange("G r n -> r G n").bitcast(I32),
+            )
+
+        def quantize(codes, scales, packed):
+            nc.vector.quantize_mx(out=codes.bitcast(FP8X4), scales=scales, in_=packed.rearrange("p n t -> p (n t)"))
+
+        def widen_x(j):
+            i = min(j, len(X_LOADS) - 1)
+            values = xb[i][:, j - X_LOADS[i][0], :].bitcast(FP8)
+            for b in range(X_BLOCKS):
+                cols = slice(X_BLOCK * b, X_BLOCK * (b + 1))
+                scale = xs[:, j, b : b + 1]
+                if b < X_BLOCKS // 2:
+                    nc.vector.tensor_scalar(out=x_rows[j][:, cols], in0=values[:, cols], scalar1=scale, scalar2=None, op0=ALU.mult)
+                else:
+                    nc.scalar.activation(out=x_rows[j][:, cols], in_=values[:, cols], func=ACT.Copy, scale=scale)
+
+        def turn(rows, passes, into):
+            words = rows.bitcast(F32)
+            for g in range(passes):
+                for u in range(2):
+                    c = P * (2 * g + u)
+                    nc.tensor.transpose(into[:, c : c + P], words[:, 2 * P * g + u : 2 * P * (g + 1) : 2], ident[:])
+
+        def turned_x_out(j, engine_copy):
+            engine_copy(out=x_turned[j][:].bitcast(F32), in_=bank[j][:].rearrange("p (g u r) -> p g r u", g=X_PASSES, u=2))
+
+        def quantize_x(j):
+            cols = slice(P * j, P * (j + 1))
+            for g in range(X_PASSES):
+                quantize(x_codes[g][:, cols], x_scales[g][:, cols], x_turned[j][:, g])
+
+        def order_gate_words(G, t0=0, t1=PACK):
+            nc.vector.tensor_copy(
+                out=gw[G][:].rearrange("p t g n -> p t (g n)").rearrange("p t (c b) -> p t c b", b=FP4_WORD)[:, t0:t1],
+                in_=gw_raw[G][:].rearrange("p g n -> p (g n)").rearrange("p (c t b) -> p t c b", t=PACK, b=FP4_WORD)[:, t0:t1],
+            )
+
+        def encode(plane):
+            G, t = divmod(plane, PACK)
+            for g in range(X_PASSES):
+                nc.tensor.matmul_mx(
+                    out=bank[U_BANKS[t % 2]][:],
+                    lhsT=gw[G][:, t, g, :].bitcast(FP4X4),
+                    lhsT_scale=gs_first[:, g, t, :] if G == 0 else gs_rest[g][:, G - 1, t, :],
+                    rhs=x_codes[g][:].bitcast(FP8X4),
+                    rhs_scale=x_scales[g][:],
+                    start=(g == 0),
+                    stop=(g == X_PASSES - 1),
+                )
+
+        def activate(G, t):
+            u = bank[U_BANKS[t % 2]][:]
+            one = slice(t, t + 1)
+            nc.scalar.activation(out=a_abs[G][t][:], in_=u, func=ACT.Relu, scale=abs_gain[:, G, one], bias=a_bias[:, G, one])
+            nc.scalar.activation(out=m_abs[G // 2][:, t, G % 2, :], in_=u, func=ACT.Relu, scale=m_scale[:, G, one], bias=m_bias[:, G, one])
+
+        def sign_a(G, t):
+            nc.vector.tensor_scalar(out=a_planes[G][:, t, :], in0=a_abs[G][t][:], scalar1=sign_gain[:, G, t : t + 1], scalar2=None, op0=ALU.mult)
+
+        def make_gate(G, t):
+            nc.vector.tensor_scalar(
+                out=gate[G // 2][:, t, G % 2, :], in0=a_abs[G][t][:],
+                scalar1=0.0, scalar2=sign_gain[:, G, t : t + 1], op0=ALU.is_gt, op1=ALU.mult,
+            )
+
+        def pack_on_vector(packed, planes):
+            nc.vector.tensor_copy(out=packed.rearrange("p (c i) t -> p c t i", i=4), in_=planes.rearrange("p t (c i) -> p c t i", i=4))
+
+        def pack_on_scalar(packed, planes):
+            nc.scalar.copy(out=packed, in_=planes.rearrange("p t n -> p n t"))
+
+        def pack_a(G, tokens):
+            pack_on_vector(a_packed[G][:, tokens, :], a_planes[G][:, :, tokens])
+
+        def quantize_a(G, tokens):
+            quantize(a_codes[G][:, tokens], a_scales[G][:, tokens], a_packed[G][:, tokens, :])
+
+        def gate_f(j, pair, tiles=1):
+            def by_tile(planes):
+                return planes.rearrange("p t G n -> p (t G) n")[:, :, P * j : P * (j + tiles)].rearrange("p c (j r) -> p c j r", r=P)
+
+            nc.vector.tensor_tensor(
+                out=f_planes[pair][:, j : j + tiles].rearrange("p j t G r -> p (t G) j r"),
+                in0=by_tile(gate[pair][:]), in1=by_tile(m_abs[pair][:]), op=ALU.mult,
+            )
+
+        def pack_f(j, pair, pack=pack_on_vector):
+            pack(f_packed[j][pair][:], f_planes[pair][:, j].rearrange("p t G r -> p t (G r)"))
+
+        def quantize_f(j, pair):
+            quantize(f_codes[j][pair][:], f_scales[j][pair][:], f_packed[j][pair][:])
+
+        def decode(o, j, G, d0, acc):
+            if o == XAUX:
+                codes, scales, c = a_codes[G], a_scales[G], P * j
+            else:
+                codes, scales, c = f_codes[j][G // 2], f_scales[j][G // 2], P * (G % 2)
+            d1 = d0 + acc.shape[1]
+            nc.tensor.matmul_mx(
+                out=acc,
+                lhsT=codes[:, c : c + P].bitcast(FP8X4),
+                lhsT_scale=scales[:, c : c + P],
+                rhs=dw[G][:, FP4_WORD * d0 : FP4_WORD * d1].bitcast(FP4X4),
+                rhs_scale=ds[:, G, d0:d1],
+                start=(G == 0),
+                stop=(G == GROUPS - 1),
+            )
+
+        def decode_half(o, j, h, groups):
+            for G in groups:
+                decode(o, j, G, BANK * h, bank[2 * j + h][:])
+
+        outs = [out.rearrange("(r j) d -> j r d", j=TILES) for out in (out_0, out_1)]
+
+        def store(o, j, d0, acc, engine_copy):
+            h, c0 = divmod(d0, BANK)
+            staged = result[o][j][h][:, c0 : c0 + acc.shape[1]]
+            engine_copy(out=staged, in_=acc)
+            nc.sync.dma_start(out=outs[o][j][:, d0 : d0 + acc.shape[1]], in_=staged)
+
+        def store_half(o, j, h):
+            store(o, j, BANK * h, bank[2 * j + h][:], nc.scalar.copy)
+
+        widen_x(0)
+        turn(x_rows[0][:], X_PASSES, bank[0])
+        widen_x(1)
+        warm_up(WARMUP_MATMULS[1])
+        turn(x_rows[1][:], X_PASSES, bank[1])
+        widen_x(2)
+        turn(x_rows[2][:], X_PASSES, bank[2])
+        turned_x_out(0, nc.vector.tensor_copy)
+        widen_x(3)
+        turn(vec_rows[:], 1, bank[VECTOR_BANK])
+        turn(x_rows[3][:], X_PASSES, bank[3])
+        warm_up(WARMUP_MATMULS[2])
+        for j in range(1, TILES):
+            turned_x_out(j, nc.scalar.copy)
+        nc.scalar.copy(
+            out=vec[:].rearrange("p v G t -> p (v G) t").bitcast(F32),
+            in_=bank[VECTOR_BANK][:, 0 : 2 * P].rearrange("p (u r) -> p r u", u=2)[:, 0 : len(vectors) * GROUPS, :],
+        )
+        nc.scalar.activation(out=abs_gain[:], in_=gain, func=ACT.Abs)
+        nc.scalar.activation(out=exp_mag[:], in_=log_mag, func=ACT.Exp)
+        nc.scalar.activation(out=sign_gain[:], in_=gain, func=ACT.Sign)
+        quantize_x(0)
+        order_gate_words(0, 0, PACK // 2)
+        quantize_x(1)
+        nc.vector.tensor_copy(out=gs_first[:], in_=gs_first_raw[:].rearrange("p g (m t) -> p g t m", t=PACK))
+        quantize_x(2)
+        quantize_x(3)
+        nc.vector.tensor_tensor(out=a_bias[:], in0=abs_gain[:], in1=gate_bias, op=ALU.mult)
+        nc.vector.tensor_tensor(out=m_scale[:], in0=abs_gain[:], in1=exp_mag[:], op=ALU.mult)
+        nc.vector.tensor_tensor(out=m_bias[:], in0=abs_gain[:], in1=mag_bias, op=ALU.mult)
+        order_gate_words(0, PACK // 2, PACK)
+
+        nc.vector.tensor_copy(out=gs_rest[0][:], in_=gs_rest_raw[:].rearrange("p (G m t) -> p G t m", t=PACK, m=P))
+        for Q in range(QUADRANTS):
+            nc.sync.dma_start(
+                out=gs_rest[1][32 * Q : 32 * Q + PACK].rearrange("p G t m -> p (G t m)").bitcast(I32),
+                in_=gs_rest[0][32 * Q + PACK : 32 * Q + 2 * PACK].rearrange("p G t m -> p (G t m)").bitcast(I32),
             )
         for G in range(GROUPS):
             nc.sync.dma_start(out=dw[G][:].bitcast(I32), in_=w_dec_words[G].bitcast(I32))
 
-        def widen(j):
-            src = xb[j // 2][:, j % 2, :].bitcast(FP8)
-            for b in range(XBLOCKS):
-                cols = slice(128 * b, 128 * (b + 1))
-                if b < VEC_BLOCKS:
-                    nc.vector.tensor_scalar(out=xw[j][:, cols], in0=src[:, cols], scalar1=xs[:, j, b : b + 1], scalar2=None, op0=ALU.mult)
-                else:
-                    nc.scalar.activation(out=xw[j][:, cols], in_=src[:, cols], func=ACT.Copy, scale=xs[:, j, b : b + 1])
-
-        def turn(j):
-            words = xw[j][:].bitcast(F32)
-            for g in range(XPASS):
-                for u in range(2):
-                    c = 128 * (2 * g + u)
-                    nc.tensor.transpose(bank[j][:, c : c + 128], words[:, 256 * g + u : 256 * (g + 1) : 2], ident[:])
-
-        def turn_out(j):
-            nc.scalar.copy(
-                out=xg[j][:].bitcast(F32),
-                in_=bank[j][:].rearrange("p (g u r) -> p g r u", g=XPASS, u=2),
-            )
-
-        def quantize(codes, scales, src):
-            nc.vector.quantize_mx(out=codes.bitcast(FP8X4), scales=scales, in_=src)
-
-        def quant_x(j):
-            for g in range(XPASS):
-                cols = slice(128 * j, 128 * (j + 1))
-                quantize(xq[g][:, cols], xqs[g][:, cols], xg[j][:, g].rearrange("p r t -> p (r t)"))
-
-        def perm_words(G):
-            nc.vector.tensor_copy(
-                out=gw[G][:].rearrange("p t g n -> p t (g n)").rearrange("p t (c b) -> p t c b", b=2),
-                in_=gw_raw[G][:].rearrange("p g n -> p (g n)").rearrange("p (c t b) -> p t c b", t=PACK, b=2),
-            )
-
-        def perm_scales(G):
-            nc.vector.tensor_copy(
-                out=gs[G][:],
-                in_=gs_raw[G // 2][:, :, 512 * (G % 2) : 512 * (G % 2 + 1)].rearrange("p g (m t) -> p t g m", t=PACK),
-            )
-
-        def encode(G, t):
-            u = bank[U_BANKS[t % 2]]
-            for g in range(XPASS):
-                nc.tensor.matmul_mx(
-                    out=u[:], lhsT=gw[G][:, t, g, :].bitcast(FP4X4), lhsT_scale=gs[G][:, t, g, :],
-                    rhs=xq[g][:].bitcast(FP8X4), rhs_scale=xqs[g][:], start=(g == 0), stop=(g == XPASS - 1),
-                )
-
-        def activate(G, t):
-            u = bank[U_BANKS[t % 2]]
-            nc.scalar.activation(out=a_abs[G][t][:], in_=u[:], func=ACT.Relu, scale=ag[:, G, t : t + 1], bias=a_bias[:, G, t : t + 1])
-            nc.scalar.activation(out=m_abs[G // 2][:, t, G % 2, :], in_=u[:], func=ACT.Relu, scale=m_scale[:, G, t : t + 1], bias=m_bias[:, G, t : t + 1])
-
-        def signs(G, t):
-            nc.vector.tensor_scalar(out=a_pl[G][:, t, :], in0=a_abs[G][t][:], scalar1=sg[:, G, t : t + 1], scalar2=None, op0=ALU.mult)
-            nc.vector.tensor_scalar(out=gate[G // 2][:, t, G % 2, :], in0=a_abs[G][t][:], scalar1=0.0, scalar2=sg[:, G, t : t + 1], op0=ALU.is_gt, op1=ALU.mult)
-
-        def interleave(dst, src, on_scalar=False):
-            out = dst.rearrange("p (c i) t -> p c t i", i=4)
-            in_ = src.rearrange("p t (c i) -> p c t i", i=4)
-            if on_scalar:
-                nc.scalar.copy(out=out, in_=in_)
-            else:
-                nc.vector.tensor_copy(out=out, in_=in_)
-
-        def il_a(G, n0=0, n1=N):
-            interleave(a_il[G][:, n0:n1, :], a_pl[G][:, :, n0:n1])
-
-        def quant_a(G, n0=0, n1=N):
-            quantize(aq[G][:, n0:n1], aqs[G][:, n0:n1], a_il[G][:, n0:n1, :].rearrange("p n t -> p (n t)"))
-
-        def gate_f(j, gh):
-            cols = slice(P * j, P * (j + 1))
-            nc.vector.tensor_tensor(out=f_pl[j][gh][:], in0=gate[gh][:, :, :, cols], in1=m_abs[gh][:, :, :, cols], op=ALU.mult)
-
-        def il_f(j, gh, on_scalar=False):
-            interleave(f_il[j][gh][:], f_pl[j][gh][:].rearrange("p t g r -> p t (g r)"), on_scalar)
-
-        def quant_f(j, gh):
-            quantize(fq[j][gh][:], fqs[j][gh][:], f_il[j][gh][:].rearrange("p n t -> p (n t)"))
-
-        def decode(o, j, h, G):
-            if o == 1:
-                codes, scales = aq[G][:, P * j : P * (j + 1)], aqs[G][:, P * j : P * (j + 1)]
-            else:
-                c = P * (G % 2)
-                codes, scales = fq[j][G // 2][:, c : c + P], fqs[j][G // 2][:, c : c + P]
-            nc.tensor.matmul_mx(
-                out=bank[2 * j + h][:], lhsT=codes.bitcast(FP8X4), lhsT_scale=scales,
-                rhs=dw[G][:, 1024 * h : 1024 * (h + 1)].bitcast(FP4X4), rhs_scale=ds[:, G, 512 * h : 512 * (h + 1)],
-                start=(G == 0), stop=(G == GROUPS - 1),
-            )
-
-        outs = [o.rearrange("(p j) d -> j p d", j=TILES) for o in (out_0, out_1)]
-
-        def finish(o, j, h, on_vector=False):
-            if on_vector:
-                nc.vector.tensor_copy(out=res[o][j][h][:], in_=bank[2 * j + h][:])
-            else:
-                nc.scalar.copy(out=res[o][j][h][:], in_=bank[2 * j + h][:])
-            nc.sync.dma_start(out=outs[o][j][:, 512 * h : 512 * (h + 1)], in_=res[o][j][h][:])
-
-        def keep_warm():
-            nc.tensor.matmul(bank[7][:], lhsT=zeros[:, 0:P], rhs=zeros[:], start=True, stop=True)
-
-        widen(0)
-        turn(0)
-        widen(1)
-        turn(1)
-        keep_warm()
-        widen(2)
-        turn(2)
-        turn_out(0)
-        widen(3)
-        turn(3)
-        keep_warm()
-        turn_out(1)
-        turn_out(2)
-        turn_out(3)
-        nc.scalar.activation(out=er[:], in_=vr[:], func=ACT.Exp)
-        nc.scalar.activation(out=ag[:], in_=vg[:], func=ACT.Abs)
-        nc.scalar.activation(out=sg[:], in_=vg[:], func=ACT.Sign)
-        perm_words(0)
-        quant_x(0)
-        perm_scales(0)
-        quant_x(1)
-        quant_x(2)
-        quant_x(3)
-        nc.vector.tensor_tensor(out=a_bias[:], in0=ag[:], in1=vb[:], op=ALU.mult)
-        nc.vector.tensor_tensor(out=m_scale[:], in0=ag[:], in1=er[:], op=ALU.mult)
-        nc.vector.tensor_tensor(out=m_bias[:], in0=ag[:], in1=vm[:], op=ALU.mult)
-        perm_words(1)
-        perm_scales(1)
-
-        fill = {
-            (0, 1): [lambda: perm_words(2)], (0, 2): [lambda: perm_scales(2)], (0, 3): [lambda: perm_scales(3)],
-            (1, 2): [lambda: perm_words(3)],
-            (2, 2): [lambda: gate_f(0, 0)], (2, 3): [lambda: gate_f(1, 0)],
-            (3, 2): [lambda: gate_f(2, 0)], (3, 3): [lambda: gate_f(3, 0)],
-        }
-        early = [(j, h) for j in range(TILES - 1) for h in range(HALVES)]
-        last = TILES - 1
-        encode(0, 0)
-        encode(0, 1)
+        other_work = (
+            lambda: order_gate_words(2),
+            lambda: order_gate_words(3),
+            lambda: gate_f(0, 0, TILES // 2),
+            lambda: gate_f(TILES // 2, 0, TILES // 2),
+        )
+        first_tokens, second_tokens = slice(0, N // 2), slice(N // 2, N)
+        encode(0)
+        encode(1)
+        order_gate_words(1)
         for G in range(GROUPS):
             for t in range(PACK):
                 activate(G, t)
-                for work in fill.get((G, t), []):
-                    work()
-                signs(G, t)
-                if t == 0 and G > 0:
-                    quant_a(G - 1)
-                if t == PACK - 1 and G < GROUPS - 1:
-                    il_a(G)
-                s = PACK * G + t + 2
-                if s < PACK * GROUPS:
-                    encode(s // PACK, s % PACK)
-                if G > 0 and t > 0:
-                    for j, h in early[2 * (t - 1) : 2 * t]:
-                        decode(1, j, h, G - 1)
+                if t == 1:
+                    other_work[G]()
+                if t == PACK - 2:
+                    for done in range(PACK - 1):
+                        sign_a(G, done)
+                    make_gate(G, 0)
+                if t == PACK - 1:
+                    sign_a(G, t)
+                    make_gate(G, 1)
+                    pack_a(G, first_tokens)
+                    make_gate(G, 2)
+                    quantize_a(G, first_tokens)
+                    pack_a(G, second_tokens)
+                    make_gate(G, 3)
+                    quantize_a(G, second_tokens)
+                ahead = PACK * G + t + len(U_BANKS)
+                if ahead < PACK * GROUPS:
+                    encode(ahead)
+                if G > 0 and t < LAST:
+                    for h in range(HALVES):
+                        decode_half(XAUX, t, h, [G - 1])
 
-        G = GROUPS - 1
         for h in range(HALVES):
-            for g in range(GROUPS - 1):
-                decode(1, last, h, g)
-        il_f(0, 0, on_scalar=True)
-        il_a(G, 0, N // 2)
-        il_a(G, N // 2, N)
-        quant_a(G, 0, N // 2)
-        gate_f(0, 1)
-        quant_a(G, N // 2, N)
+            decode_half(XAUX, LAST, h, range(GROUPS - 1))
+        pack_f(0, 0, pack_on_scalar)
         for j in range(TILES):
             for h in range(HALVES):
-                decode(1, j, h, G)
-                finish(1, j, h)
-        il_f(0, 1)
-        quant_f(0, 0)
+                decode_half(XAUX, j, h, [GROUPS - 1])
+                store_half(XAUX, j, h)
+            if j == 1:
+                pack_f(1, 0, pack_on_scalar)
+
+        f_steps = (
+            ((gate_f, 0, 1), (quantize_f, 0, 0), (pack_f, 0, 1), (gate_f, 1, 1), (quantize_f, 0, 1), (pack_f, 1, 1), (quantize_f, 1, 0)),
+            ((pack_f, 2, 0), (quantize_f, 1, 1), (gate_f, 2, 1), (quantize_f, 2, 0), (pack_f, 2, 1)),
+            ((gate_f, 3, 1), (quantize_f, 2, 1), (pack_f, 3, 1), (quantize_f, 3, 0)),
+            ((quantize_f, 3, 1),),
+        )
         for j in range(TILES):
-            if j < last:
-                il_f(j + 1, 0)
-            quant_f(j, 1)
-            if j < last:
-                gate_f(j + 1, 1)
-                quant_f(j + 1, 0)
-                il_f(j + 1, 1)
-            for h in range(HALVES):
-                for g in range(GROUPS):
-                    decode(0, j, h, g)
-                finish(0, j, h, on_vector=(j == last and h == 1))
+            for step, tile_index, pair in f_steps[j]:
+                step(tile_index, pair)
+            if j < LAST:
+                for h in range(HALVES):
+                    decode_half(XHAT, j, h, range(2))
+                for h in range(HALVES):
+                    decode_half(XHAT, j, h, range(2, GROUPS))
+                    store_half(XHAT, j, h)
+                    if j == 1 and h == 0:
+                        pack_f(LAST, 0, pack_on_scalar)
+
+        decode_half(XHAT, LAST, 0, range(GROUPS))
+        store_half(XHAT, LAST, 0)
+        for q in range(BANK // P):
+            d0, acc = BANK + P * q, bank[q][:, 0:P]
+            for G in range(GROUPS):
+                decode(XHAT, LAST, G, d0, acc)
+            store(XHAT, LAST, d0, acc, nc.vector.tensor_copy if q % 2 == 0 else nc.scalar.copy)

@@ -30,13 +30,14 @@ PAIRS = GROUPS // 2
 HALVES = D // BANK
 X_BLOCK = 128
 X_BLOCKS = D // X_BLOCK
+X_BLOCKS_ON_VECTOR = 3
 X_LOADS = ((0, 1), (1, 1), (2, 2))
 XHAT, XAUX = 0, 1
 LAST = TILES - 1
 
 U_BANKS = (2 * LAST, 2 * LAST + 1)
 VECTOR_BANK = TILES
-WARMUP_MATMULS = (9, 2, 3)
+WARMUP_MATMULS = (5, 2, 3)
 
 
 def tile_gatedsparseautoencoderwithaux_d1p_kernel(
@@ -57,7 +58,7 @@ def tile_gatedsparseautoencoderwithaux_d1p_kernel(
         xs = tile([P, TILES, X_BLOCKS], F32, "xs")
         xb = [tile([P, n, D], U8, "xbytes%d" % i) for i, (j0, n) in enumerate(X_LOADS)]
         x_rows = [tile([P, D], BF16, "x_rows%d" % j) for j in range(TILES)]
-        x_turned = [tile([P, X_PASSES, P, PACK], BF16, "x_turned%d" % j) for j in range(TILES)]
+        x_turned = [tile([P, X_PASSES, 2, P, PACK], BF16, "x_turned%d" % i) for i in range(TILES // 2)]
         x_codes = [tile([P, N], U32, "x_codes%d" % g) for g in range(X_PASSES)]
         x_scales = [tile([P, N], U8, "x_scales%d" % g) for g in range(X_PASSES)]
         ident = tile([P, P], F32, "ident")
@@ -100,37 +101,37 @@ def tile_gatedsparseautoencoderwithaux_d1p_kernel(
             for o in (XHAT, XAUX)
         ]
 
-        nc.vector.memset(gs_first_raw[:].rearrange("p g n -> p (g n)").bitcast(I32), 0)
-        nc.vector.memset(zeros[:], 0.0)
-        nc.vector.memset(vec_rows[:], 0.0)
-        nc.vector.memset(gs_rest_raw[:].bitcast(I32), 0)
-        nc.vector.memset(gs_rest[1][:].rearrange("p G t m -> p (G t m)").bitcast(I32), 0)
-        nc.vector.memset(ds[:].rearrange("p G n -> p (G n)").bitcast(I32), 0)
         make_identity(nc, ident[:])
+        nc.sync.dma_start(out=xs[:], in_=x_scale.rearrange("(r j) b -> r j b", j=TILES))
+        for i, (j0, n) in enumerate(X_LOADS):
+            nc.sync.dma_start(out=xb[i][:], in_=x_bytes.rearrange("(r j) k -> r j k", j=TILES)[:, j0 : j0 + n, :])
+
+        nc.vector.memset(zeros[:], 0.0)
+        nc.scalar.activation(out=table_warmup[:], in_=zeros[:, 0:1], func=ACT.Exp)
 
         def warm_up(matmuls):
             for i in range(matmuls):
                 nc.tensor.matmul(bank[U_BANKS[1]][:], lhsT=zeros[:, 0:P], rhs=zeros[:], start=True, stop=True)
 
-        nc.scalar.activation(out=table_warmup[:], in_=zeros[:, 0:1], func=ACT.Exp)
         warm_up(WARMUP_MATMULS[0])
 
-        nc.sync.dma_start(out=xs[:], in_=x_scale.rearrange("(r j) b -> r j b", j=TILES))
-        for i, (j0, n) in enumerate(X_LOADS):
-            nc.sync.dma_start(out=xb[i][:], in_=x_bytes.rearrange("(r j) k -> r j k", j=TILES)[:, j0 : j0 + n, :])
+        nc.vector.memset(gs_first_raw[:].rearrange("p g n -> p (g n)").bitcast(I32), 0)
+        nc.vector.memset(vec_rows[:], 0.0)
+        nc.vector.memset(gs_rest_raw[:].bitcast(I32), 0)
+        nc.vector.memset(ds[:].rearrange("p G n -> p (G n)").bitcast(I32), 0)
 
         def load_gate_words(G):
             cols = slice(K_PASS * FP4_WORD * G, K_PASS * FP4_WORD * (G + 1))
             nc.sync.dma_start(out=gw_raw[G][:].bitcast(I32), in_=w_gate_words.rearrange("g p n -> p g n")[:, :, cols].bitcast(I32))
 
         load_gate_words(0)
-        for i, v in enumerate(vectors):
-            nc.sync.dma_start(out=vec_rows[GROUPS * i : GROUPS * (i + 1), :], in_=v.rearrange("(G n) -> G n", G=GROUPS))
         for Q in range(QUADRANTS):
             nc.sync.dma_start(
                 out=gs_first_raw[32 * Q : 32 * Q + PACK].bitcast(I32),
                 in_=w_gate_scales[:, PACK * Q : PACK * (Q + 1), 0:K_PASS].rearrange("g r n -> r g n").bitcast(I32),
             )
+        for i, v in enumerate(vectors):
+            nc.sync.dma_start(out=vec_rows[GROUPS * i : GROUPS * (i + 1), :], in_=v.rearrange("(G n) -> G n", G=GROUPS))
         for Q in range(QUADRANTS):
             nc.sync.dma_start(
                 out=gs_rest_raw[32 * Q : 32 * Q + X_PASSES * PACK].bitcast(I32),
@@ -153,7 +154,7 @@ def tile_gatedsparseautoencoderwithaux_d1p_kernel(
             for b in range(X_BLOCKS):
                 cols = slice(X_BLOCK * b, X_BLOCK * (b + 1))
                 scale = xs[:, j, b : b + 1]
-                if b < X_BLOCKS // 2:
+                if b < X_BLOCKS_ON_VECTOR:
                     nc.vector.tensor_scalar(out=x_rows[j][:, cols], in0=values[:, cols], scalar1=scale, scalar2=None, op0=ALU.mult)
                 else:
                     nc.scalar.activation(out=x_rows[j][:, cols], in_=values[:, cols], func=ACT.Copy, scale=scale)
@@ -166,12 +167,12 @@ def tile_gatedsparseautoencoderwithaux_d1p_kernel(
                     nc.tensor.transpose(into[:, c : c + P], words[:, 2 * P * g + u : 2 * P * (g + 1) : 2], ident[:])
 
         def turned_x_out(j, engine_copy):
-            engine_copy(out=x_turned[j][:].bitcast(F32), in_=bank[j][:].rearrange("p (g u r) -> p g r u", g=X_PASSES, u=2))
+            engine_copy(out=x_turned[j // 2][:, :, j % 2].bitcast(F32), in_=bank[j][:].rearrange("p (g u r) -> p g r u", g=X_PASSES, u=2))
 
-        def quantize_x(j):
-            cols = slice(P * j, P * (j + 1))
+        def quantize_x(i):
+            cols = slice(2 * P * i, 2 * P * (i + 1))
             for g in range(X_PASSES):
-                quantize(x_codes[g][:, cols], x_scales[g][:, cols], x_turned[j][:, g])
+                quantize(x_codes[g][:, cols], x_scales[g][:, cols], x_turned[i][:, g].rearrange("p j r t -> p (j r) t"))
 
         def order_gate_words(G, t0=0, t1=PACK):
             nc.vector.tensor_copy(
@@ -207,14 +208,11 @@ def tile_gatedsparseautoencoderwithaux_d1p_kernel(
                 scalar1=0.0, scalar2=sign_gain[:, G, t : t + 1], op0=ALU.is_gt, op1=ALU.mult,
             )
 
-        def pack_on_vector(packed, planes):
-            nc.vector.tensor_copy(out=packed.rearrange("p (c i) t -> p c t i", i=4), in_=planes.rearrange("p t (c i) -> p c t i", i=4))
-
-        def pack_on_scalar(packed, planes):
-            nc.scalar.copy(out=packed, in_=planes.rearrange("p t n -> p n t"))
+        def pack(packed, planes, engine_copy):
+            engine_copy(out=packed.rearrange("p (c i) t -> p c t i", i=4), in_=planes.rearrange("p t (c i) -> p c t i", i=4))
 
         def pack_a(G, tokens):
-            pack_on_vector(a_packed[G][:, tokens, :], a_planes[G][:, :, tokens])
+            pack(a_packed[G][:, tokens, :], a_planes[G][:, :, tokens], nc.vector.tensor_copy)
 
         def quantize_a(G, tokens):
             quantize(a_codes[G][:, tokens], a_scales[G][:, tokens], a_packed[G][:, tokens, :])
@@ -228,8 +226,8 @@ def tile_gatedsparseautoencoderwithaux_d1p_kernel(
                 in0=by_tile(gate[pair][:]), in1=by_tile(m_abs[pair][:]), op=ALU.mult,
             )
 
-        def pack_f(j, pair, pack=pack_on_vector):
-            pack(f_packed[j][pair][:], f_planes[pair][:, j].rearrange("p t G r -> p t (G r)"))
+        def pack_f(j, pair, engine_copy=nc.vector.tensor_copy):
+            pack(f_packed[j][pair][:], f_planes[pair][:, j].rearrange("p t G r -> p t (G r)"), engine_copy)
 
         def quantize_f(j, pair):
             quantize(f_codes[j][pair][:], f_scales[j][pair][:], f_packed[j][pair][:])
@@ -272,10 +270,10 @@ def tile_gatedsparseautoencoderwithaux_d1p_kernel(
         turn(x_rows[1][:], X_PASSES, bank[1])
         widen_x(2)
         turn(x_rows[2][:], X_PASSES, bank[2])
-        turned_x_out(0, nc.vector.tensor_copy)
         widen_x(3)
-        turn(vec_rows[:], 1, bank[VECTOR_BANK])
+        turned_x_out(0, nc.vector.tensor_copy)
         turn(x_rows[3][:], X_PASSES, bank[3])
+        turn(vec_rows[:], 1, bank[VECTOR_BANK])
         warm_up(WARMUP_MATMULS[2])
         for j in range(1, TILES):
             turned_x_out(j, nc.scalar.copy)
@@ -286,17 +284,15 @@ def tile_gatedsparseautoencoderwithaux_d1p_kernel(
         nc.scalar.activation(out=abs_gain[:], in_=gain, func=ACT.Abs)
         nc.scalar.activation(out=exp_mag[:], in_=log_mag, func=ACT.Exp)
         nc.scalar.activation(out=sign_gain[:], in_=gain, func=ACT.Sign)
-        quantize_x(0)
-        order_gate_words(0, 0, PACK // 2)
-        quantize_x(1)
+        order_gate_words(0)
         nc.vector.tensor_copy(out=gs_first[:], in_=gs_first_raw[:].rearrange("p g (m t) -> p g t m", t=PACK))
-        quantize_x(2)
-        quantize_x(3)
+        quantize_x(0)
+        quantize_x(1)
         nc.vector.tensor_tensor(out=a_bias[:], in0=abs_gain[:], in1=gate_bias, op=ALU.mult)
         nc.vector.tensor_tensor(out=m_scale[:], in0=abs_gain[:], in1=exp_mag[:], op=ALU.mult)
         nc.vector.tensor_tensor(out=m_bias[:], in0=abs_gain[:], in1=mag_bias, op=ALU.mult)
-        order_gate_words(0, PACK // 2, PACK)
 
+        nc.vector.memset(gs_rest[1][:].rearrange("p G t m -> p (G t m)").bitcast(I32), 0)
         nc.vector.tensor_copy(out=gs_rest[0][:], in_=gs_rest_raw[:].rearrange("p (G m t) -> p G t m", t=PACK, m=P))
         for Q in range(QUADRANTS):
             nc.sync.dma_start(
@@ -306,55 +302,56 @@ def tile_gatedsparseautoencoderwithaux_d1p_kernel(
         for G in range(GROUPS):
             nc.sync.dma_start(out=dw[G][:].bitcast(I32), in_=w_dec_words[G].bitcast(I32))
 
-        other_work = (
-            lambda: order_gate_words(2),
-            lambda: order_gate_words(3),
-            lambda: gate_f(0, 0, TILES // 2),
-            lambda: gate_f(TILES // 2, 0, TILES // 2),
-        )
-        first_tokens, second_tokens = slice(0, N // 2), slice(N // 2, N)
+        extra_work = {
+            (0, 1): lambda: order_gate_words(2),
+            (0, 2): lambda: order_gate_words(3, 0, PACK // 2),
+            (1, 1): lambda: order_gate_words(3, PACK // 2, PACK),
+            (2, 1): lambda: gate_f(0, 0, TILES // 2),
+            (3, 1): lambda: gate_f(TILES // 2, 0, TILES // 2),
+        }
+        whole, first_tokens, second_tokens = slice(0, N), slice(0, N // 2), slice(N // 2, N)
+        in_halves = range(GROUPS - 2, GROUPS)
         encode(0)
         encode(1)
         order_gate_words(1)
         for G in range(GROUPS):
             for t in range(PACK):
                 activate(G, t)
-                if t == 1:
-                    other_work[G]()
-                if t == PACK - 2:
-                    for done in range(PACK - 1):
-                        sign_a(G, done)
-                    make_gate(G, 0)
-                if t == PACK - 1:
-                    sign_a(G, t)
-                    make_gate(G, 1)
+                if (G, t) in extra_work:
+                    extra_work[G, t]()
+                sign_a(G, t)
+                make_gate(G, t)
+                if t == 0 and G > 0:
+                    quantize_a(G - 1, second_tokens if G - 1 in in_halves else whole)
+                if t == PACK - 1 and G in in_halves:
                     pack_a(G, first_tokens)
-                    make_gate(G, 2)
-                    quantize_a(G, first_tokens)
                     pack_a(G, second_tokens)
-                    make_gate(G, 3)
-                    quantize_a(G, second_tokens)
+                    quantize_a(G, first_tokens)
+                elif t == PACK - 1:
+                    pack_a(G, whole)
                 ahead = PACK * G + t + len(U_BANKS)
                 if ahead < PACK * GROUPS:
                     encode(ahead)
-                if G > 0 and t < LAST:
+                j = t if G - 1 in in_halves else t - 1
+                if G > 0 and 0 <= j < LAST:
                     for h in range(HALVES):
-                        decode_half(XAUX, t, h, [G - 1])
+                        decode_half(XAUX, j, h, [G - 1])
+        gate_f(0, 1)
+        quantize_a(GROUPS - 1, second_tokens)
 
         for h in range(HALVES):
             decode_half(XAUX, LAST, h, range(GROUPS - 1))
-        pack_f(0, 0, pack_on_scalar)
+        pack_f(0, 0, nc.scalar.copy)
+        pack_f(1, 0, nc.scalar.copy)
         for j in range(TILES):
             for h in range(HALVES):
                 decode_half(XAUX, j, h, [GROUPS - 1])
                 store_half(XAUX, j, h)
-            if j == 1:
-                pack_f(1, 0, pack_on_scalar)
 
         f_steps = (
-            ((gate_f, 0, 1), (quantize_f, 0, 0), (pack_f, 0, 1), (gate_f, 1, 1), (quantize_f, 0, 1), (pack_f, 1, 1), (quantize_f, 1, 0)),
+            ((quantize_f, 0, 0), (pack_f, 0, 1), (gate_f, 1, 1), (quantize_f, 0, 1), (pack_f, 1, 1), (quantize_f, 1, 0)),
             ((pack_f, 2, 0), (quantize_f, 1, 1), (gate_f, 2, 1), (quantize_f, 2, 0), (pack_f, 2, 1)),
-            ((gate_f, 3, 1), (quantize_f, 2, 1), (pack_f, 3, 1), (quantize_f, 3, 0)),
+            ((gate_f, 3, 1), (quantize_f, 2, 1), (pack_f, 3, 0), (pack_f, 3, 1), (quantize_f, 3, 0)),
             ((quantize_f, 3, 1),),
         )
         for j in range(TILES):
@@ -366,8 +363,6 @@ def tile_gatedsparseautoencoderwithaux_d1p_kernel(
                 for h in range(HALVES):
                     decode_half(XHAT, j, h, range(2, GROUPS))
                     store_half(XHAT, j, h)
-                    if j == 1 and h == 0:
-                        pack_f(LAST, 0, pack_on_scalar)
 
         decode_half(XHAT, LAST, 0, range(GROUPS))
         store_half(XHAT, LAST, 0)

from contextlib import ExitStack

import concourse.mybir as mybir
from concourse.masks import make_identity

N, D, F = 512, 1024, 2048
FLOPS = 3 * 2 * N * D * F

F32 = mybir.dt.float32
BF16 = mybir.dt.bfloat16
I32 = mybir.dt.int32
U32 = mybir.dt.uint32
U8 = mybir.dt.uint8
FP8 = mybir.dt.float8_e4m3fn
FP8X4 = mybir.dt.float8_e4m3fn_x4
FP4X4 = mybir.dt.float4_e2m1fn_x4
ACT = mybir.ActivationFunctionType
ALU = mybir.AluOpType

P = 128
PACK = 4
K_PASS = P * PACK
BANK = 512
FP4_WORD = 2
QUADRANTS = 4
TILES = N // P
X_PASSES = D // K_PASS
GROUPS = F // K_PASS
PAIRS = GROUPS // 2
HALVES = D // BANK
X_BLOCK = 128
X_BLOCKS = D // X_BLOCK
X_BLOCKS_ON_VECTOR = 3
X_LOADS = ((0, 1), (1, 1), (2, 2))
XHAT, XAUX = 0, 1
LAST = TILES - 1

U_BANKS = (2 * LAST, 2 * LAST + 1)
VECTOR_BANK = TILES
WARMUP_MATMULS = (5, 2, 3)


def tile_gatedsparseautoencoderwithaux_d1p_kernel(
    tc, x_bytes, x_scale, w_gate_words, w_gate_scales, b_gate, r_mag, b_mag, g_feat,
    w_dec_words, w_dec_scales, out_0, out_1,
):
    nc = tc.nc
    with ExitStack() as ctx:
        sbuf = ctx.enter_context(tc.tile_pool(name="sbuf", bufs=1))
        psum = ctx.enter_context(tc.psum_pool(name="psum", bufs=1))
        ctx.enter_context(tc.manual_schedule())

        def tile(shape, dtype, name):
            return sbuf.tile(shape, dtype, name=name, align_bytes=64)

        bank = [psum.tile([P, BANK], F32, name="bank%d" % i) for i in range(TILES * HALVES)]

        xs = tile([P, TILES, X_BLOCKS], F32, "xs")
        xb = [tile([P, n, D], U8, "xbytes%d" % i) for i, (j0, n) in enumerate(X_LOADS)]
        x_rows = [tile([P, D], BF16, "x_rows%d" % j) for j in range(TILES)]
        x_turned = [tile([P, X_PASSES, 2, P, PACK], BF16, "x_turned%d" % i) for i in range(TILES // 2)]
        x_codes = [tile([P, N], U32, "x_codes%d" % g) for g in range(X_PASSES)]
        x_scales = [tile([P, N], U8, "x_scales%d" % g) for g in range(X_PASSES)]
        ident = tile([P, P], F32, "ident")

        gs_first_raw = tile([P, X_PASSES, K_PASS], U8, "gs_first_raw")
        gs_rest_raw = tile([P, F - K_PASS], U8, "gs_rest_raw")
        zeros = tile([P, BANK], BF16, "zeros")
        gw_raw = [tile([P, X_PASSES, K_PASS * FP4_WORD], U8, "gw_raw%d" % G) for G in range(GROUPS)]
        gw = [tile([P, PACK, X_PASSES, P * FP4_WORD], U8, "gw%d" % G) for G in range(GROUPS)]
        gs_first = tile([P, X_PASSES, PACK, P], U8, "gs_first")
        gs_rest = [tile([P, GROUPS - 1, PACK, P], U8, "gs_rest%d" % g) for g in range(X_PASSES)]
        dw = [tile([P, D * FP4_WORD], U8, "dw%d" % G) for G in range(GROUPS)]
        ds = tile([P, GROUPS, D], U8, "ds")

        vectors = (g_feat, r_mag, b_gate, b_mag)
        vec_rows = tile([P, K_PASS], BF16, "vec_rows")
        vec = tile([P, len(vectors), GROUPS, PACK], BF16, "vec")
        gain, log_mag, gate_bias, mag_bias = (vec[:, i] for i in range(len(vectors)))
        table_warmup = tile([P, 1], F32, "table_warmup")
        exp_mag = tile([P, GROUPS, PACK], F32, "exp_mag")
        abs_gain = tile([P, GROUPS, PACK], F32, "abs_gain")
        sign_gain = tile([P, GROUPS, PACK], F32, "sign_gain")
        a_bias = tile([P, GROUPS, PACK], F32, "a_bias")
        m_scale = tile([P, GROUPS, PACK], F32, "m_scale")
        m_bias = tile([P, GROUPS, PACK], F32, "m_bias")

        a_abs = [[tile([P, N], BF16, "a_abs%d_%d" % (G, t)) for t in range(PACK)] for G in range(GROUPS)]
        m_abs = [tile([P, PACK, 2, N], BF16, "m_abs%d" % pair) for pair in range(PAIRS)]
        gate = [tile([P, PACK, 2, N], BF16, "gate%d" % pair) for pair in range(PAIRS)]
        a_planes = [tile([P, PACK, N], BF16, "a_planes%d" % G) for G in range(GROUPS)]
        a_packed = [tile([P, N, PACK], BF16, "a_packed%d" % G) for G in range(GROUPS)]
        a_codes = [tile([P, N], U32, "a_codes%d" % G) for G in range(GROUPS)]
        a_scales = [tile([P, N], U8, "a_scales%d" % G) for G in range(GROUPS)]
        f_planes = [tile([P, TILES, PACK, 2, P], BF16, "f_planes%d" % pair) for pair in range(PAIRS)]
        f_packed = [[tile([P, 2 * P, PACK], BF16, "f_packed%d_%d" % (j, pair)) for pair in range(PAIRS)] for j in range(TILES)]
        f_codes = [[tile([P, 2 * P], U32, "f_codes%d_%d" % (j, pair)) for pair in range(PAIRS)] for j in range(TILES)]
        f_scales = [[tile([P, 2 * P], U8, "f_scales%d_%d" % (j, pair)) for pair in range(PAIRS)] for j in range(TILES)]
        result = [
            [[tile([P, BANK], F32, "result%d_%d_%d" % (o, j, h)) for h in range(HALVES)] for j in range(TILES)]
            for o in (XHAT, XAUX)
        ]

        make_identity(nc, ident[:])
        nc.sync.dma_start(out=xs[:], in_=x_scale.rearrange("(r j) b -> r j b", j=TILES))
        for i, (j0, n) in enumerate(X_LOADS):
            nc.sync.dma_start(out=xb[i][:], in_=x_bytes.rearrange("(r j) k -> r j k", j=TILES)[:, j0 : j0 + n, :])

        nc.vector.memset(zeros[:], 0.0)
        nc.scalar.activation(out=table_warmup[:], in_=zeros[:, 0:1], func=ACT.Exp)

        def warm_up(matmuls):
            for i in range(matmuls):
                nc.tensor.matmul(bank[U_BANKS[1]][:], lhsT=zeros[:, 0:P], rhs=zeros[:], start=True, stop=True)

        warm_up(WARMUP_MATMULS[0])

        nc.vector.memset(gs_first_raw[:].rearrange("p g n -> p (g n)").bitcast(I32), 0)
        nc.vector.memset(vec_rows[:], 0.0)
        nc.vector.memset(gs_rest_raw[:].bitcast(I32), 0)
        nc.vector.memset(ds[:].rearrange("p G n -> p (G n)").bitcast(I32), 0)

        def load_gate_words(G):
            cols = slice(K_PASS * FP4_WORD * G, K_PASS * FP4_WORD * (G + 1))
            nc.sync.dma_start(out=gw_raw[G][:].bitcast(I32), in_=w_gate_words.rearrange("g p n -> p g n")[:, :, cols].bitcast(I32))

        load_gate_words(0)
        for Q in range(QUADRANTS):
            nc.sync.dma_start(
                out=gs_first_raw[32 * Q : 32 * Q + PACK].bitcast(I32),
                in_=w_gate_scales[:, PACK * Q : PACK * (Q + 1), 0:K_PASS].rearrange("g r n -> r g n").bitcast(I32),
            )
        for i, v in enumerate(vectors):
            nc.sync.dma_start(out=vec_rows[GROUPS * i : GROUPS * (i + 1), :], in_=v.rearrange("(G n) -> G n", G=GROUPS))
        for Q in range(QUADRANTS):
            nc.sync.dma_start(
                out=gs_rest_raw[32 * Q : 32 * Q + X_PASSES * PACK].bitcast(I32),
                in_=w_gate_scales[:, PACK * Q : PACK * (Q + 1), K_PASS:F].bitcast(I32),
            )
        for G in range(1, GROUPS):
            load_gate_words(G)
        for Q in range(QUADRANTS):
            nc.sync.dma_start(
                out=ds[32 * Q : 32 * Q + PACK].bitcast(I32),
                in_=w_dec_scales[:, PACK * Q : PACK * (Q + 1), :].rearrange("G r n -> r G n").bitcast(I32),
            )

        def quantize(codes, scales, packed):
            nc.vector.quantize_mx(out=codes.bitcast(FP8X4), scales=scales, in_=packed.rearrange("p n t -> p (n t)"))

        def widen_x(j):
            i = min(j, len(X_LOADS) - 1)
            values = xb[i][:, j - X_LOADS[i][0], :].bitcast(FP8)
            for b in range(X_BLOCKS):
                cols = slice(X_BLOCK * b, X_BLOCK * (b + 1))
                scale = xs[:, j, b : b + 1]
                if b < X_BLOCKS_ON_VECTOR:
                    nc.vector.tensor_scalar(out=x_rows[j][:, cols], in0=values[:, cols], scalar1=scale, scalar2=None, op0=ALU.mult)
                else:
                    nc.scalar.activation(out=x_rows[j][:, cols], in_=values[:, cols], func=ACT.Copy, scale=scale)

        def turn(rows, passes, into):
            words = rows.bitcast(F32)
            for g in range(passes):
                for u in range(2):
                    c = P * (2 * g + u)
                    nc.tensor.transpose(into[:, c : c + P], words[:, 2 * P * g + u : 2 * P * (g + 1) : 2], ident[:])

        def turned_x_out(j, engine_copy):
            engine_copy(out=x_turned[j // 2][:, :, j % 2].bitcast(F32), in_=bank[j][:].rearrange("p (g u r) -> p g r u", g=X_PASSES, u=2))

        def quantize_x(i):
            cols = slice(2 * P * i, 2 * P * (i + 1))
            for g in range(X_PASSES):
                quantize(x_codes[g][:, cols], x_scales[g][:, cols], x_turned[i][:, g].rearrange("p j r t -> p (j r) t"))

        def order_gate_words(G, t0=0, t1=PACK):
            nc.vector.tensor_copy(
                out=gw[G][:].rearrange("p t g n -> p t (g n)").rearrange("p t (c b) -> p t c b", b=FP4_WORD)[:, t0:t1],
                in_=gw_raw[G][:].rearrange("p g n -> p (g n)").rearrange("p (c t b) -> p t c b", t=PACK, b=FP4_WORD)[:, t0:t1],
            )

        def encode(plane):
            G, t = divmod(plane, PACK)
            for g in range(X_PASSES):
                nc.tensor.matmul_mx(
                    out=bank[U_BANKS[t % 2]][:],
                    lhsT=gw[G][:, t, g, :].bitcast(FP4X4),
                    lhsT_scale=gs_first[:, g, t, :] if G == 0 else gs_rest[g][:, G - 1, t, :],
                    rhs=x_codes[g][:].bitcast(FP8X4),
                    rhs_scale=x_scales[g][:],
                    start=(g == 0),
                    stop=(g == X_PASSES - 1),
                )

        def activate(G, t):
            u = bank[U_BANKS[t % 2]][:]
            one = slice(t, t + 1)
            nc.scalar.activation(out=a_abs[G][t][:], in_=u, func=ACT.Relu, scale=abs_gain[:, G, one], bias=a_bias[:, G, one])
            nc.scalar.activation(out=m_abs[G // 2][:, t, G % 2, :], in_=u, func=ACT.Relu, scale=m_scale[:, G, one], bias=m_bias[:, G, one])

        def sign_a(G, t):
            nc.vector.tensor_scalar(out=a_planes[G][:, t, :], in0=a_abs[G][t][:], scalar1=sign_gain[:, G, t : t + 1], scalar2=None, op0=ALU.mult)

        def make_gate(G, t):
            nc.vector.tensor_scalar(
                out=gate[G // 2][:, t, G % 2, :], in0=a_abs[G][t][:],
                scalar1=0.0, scalar2=sign_gain[:, G, t : t + 1], op0=ALU.is_gt, op1=ALU.mult,
            )

        def pack(packed, planes, engine_copy):
            engine_copy(out=packed.rearrange("p (c i) t -> p c t i", i=4), in_=planes.rearrange("p t (c i) -> p c t i", i=4))

        def pack_a(G, tokens):
            pack(a_packed[G][:, tokens, :], a_planes[G][:, :, tokens], nc.vector.tensor_copy)

        def quantize_a(G, tokens):
            quantize(a_codes[G][:, tokens], a_scales[G][:, tokens], a_packed[G][:, tokens, :])

        def gate_f(j, pair, tiles=1):
            def by_tile(planes):
                return planes.rearrange("p t G n -> p (t G) n")[:, :, P * j : P * (j + tiles)].rearrange("p c (j r) -> p c j r", r=P)

            nc.vector.tensor_tensor(
                out=f_planes[pair][:, j : j + tiles].rearrange("p j t G r -> p (t G) j r"),
                in0=by_tile(gate[pair][:]), in1=by_tile(m_abs[pair][:]), op=ALU.mult,
            )

        def pack_f(j, pair, engine_copy=nc.vector.tensor_copy):
            pack(f_packed[j][pair][:], f_planes[pair][:, j].rearrange("p t G r -> p t (G r)"), engine_copy)

        def quantize_f(j, pair):
            quantize(f_codes[j][pair][:], f_scales[j][pair][:], f_packed[j][pair][:])

        def decode(o, j, G, d0, acc):
            if o == XAUX:
                codes, scales, c = a_codes[G], a_scales[G], P * j
            else:
                codes, scales, c = f_codes[j][G // 2], f_scales[j][G // 2], P * (G % 2)
            d1 = d0 + acc.shape[1]
            nc.tensor.matmul_mx(
                out=acc,
                lhsT=codes[:, c : c + P].bitcast(FP8X4),
                lhsT_scale=scales[:, c : c + P],
                rhs=dw[G][:, FP4_WORD * d0 : FP4_WORD * d1].bitcast(FP4X4),
                rhs_scale=ds[:, G, d0:d1],
                start=(G == 0),
                stop=(G == GROUPS - 1),
            )

        def decode_half(o, j, h, groups):
            for G in groups:
                decode(o, j, G, BANK * h, bank[2 * j + h][:])

        outs = [out.rearrange("(r j) d -> j r d", j=TILES) for out in (out_0, out_1)]

        def store(o, j, d0, acc, engine_copy):
            h, c0 = divmod(d0, BANK)
            staged = result[o][j][h][:, c0 : c0 + acc.shape[1]]
            engine_copy(out=staged, in_=acc)
            nc.sync.dma_start(out=outs[o][j][:, d0 : d0 + acc.shape[1]], in_=staged)

        def store_half(o, j, h):
            store(o, j, BANK * h, bank[2 * j + h][:], nc.scalar.copy)

        widen_x(0)
        turn(x_rows[0][:], X_PASSES, bank[0])
        widen_x(1)
        warm_up(WARMUP_MATMULS[1])
        turn(x_rows[1][:], X_PASSES, bank[1])
        widen_x(2)
        turn(x_rows[2][:], X_PASSES, bank[2])
        widen_x(3)
        turned_x_out(0, nc.vector.tensor_copy)
        turn(x_rows[3][:], X_PASSES, bank[3])
        turn(vec_rows[:], 1, bank[VECTOR_BANK])
        warm_up(WARMUP_MATMULS[2])
        for j in range(1, TILES):
            turned_x_out(j, nc.scalar.copy)
        nc.scalar.copy(
            out=vec[:].rearrange("p v G t -> p (v G) t").bitcast(F32),
            in_=bank[VECTOR_BANK][:, 0 : 2 * P].rearrange("p (u r) -> p r u", u=2)[:, 0 : len(vectors) * GROUPS, :],
        )
        nc.scalar.activation(out=abs_gain[:], in_=gain, func=ACT.Abs)
        nc.scalar.activation(out=exp_mag[:], in_=log_mag, func=ACT.Exp)
        nc.scalar.activation(out=sign_gain[:], in_=gain, func=ACT.Sign)
        order_gate_words(0)
        nc.vector.tensor_copy(out=gs_first[:], in_=gs_first_raw[:].rearrange("p g (m t) -> p g t m", t=PACK))
        quantize_x(0)
        quantize_x(1)
        nc.vector.tensor_tensor(out=a_bias[:], in0=abs_gain[:], in1=gate_bias, op=ALU.mult)
        nc.vector.tensor_tensor(out=m_scale[:], in0=abs_gain[:], in1=exp_mag[:], op=ALU.mult)
        nc.vector.tensor_tensor(out=m_bias[:], in0=abs_gain[:], in1=mag_bias, op=ALU.mult)

        nc.vector.memset(gs_rest[1][:].rearrange("p G t m -> p (G t m)").bitcast(I32), 0)
        nc.vector.tensor_copy(out=gs_rest[0][:], in_=gs_rest_raw[:].rearrange("p (G m t) -> p G t m", t=PACK, m=P))
        for Q in range(QUADRANTS):
            nc.sync.dma_start(
                out=gs_rest[1][32 * Q : 32 * Q + PACK].rearrange("p G t m -> p (G t m)").bitcast(I32),
                in_=gs_rest[0][32 * Q + PACK : 32 * Q + 2 * PACK].rearrange("p G t m -> p (G t m)").bitcast(I32),
            )
        for G in range(GROUPS):
            nc.sync.dma_start(out=dw[G][:].bitcast(I32), in_=w_dec_words[G].bitcast(I32))

        extra_work = {
            (0, 1): lambda: order_gate_words(2),
            (0, 2): lambda: order_gate_words(3, 0, PACK // 2),
            (1, 1): lambda: order_gate_words(3, PACK // 2, PACK),
            (2, 1): lambda: gate_f(0, 0, TILES // 2),
            (3, 1): lambda: gate_f(TILES // 2, 0, TILES // 2),
        }
        whole, first_tokens, second_tokens = slice(0, N), slice(0, N // 2), slice(N // 2, N)
        in_halves = range(GROUPS - 2, GROUPS)
        encode(0)
        encode(1)
        order_gate_words(1)
        for G in range(GROUPS):
            for t in range(PACK):
                activate(G, t)
                if (G, t) in extra_work:
                    extra_work[G, t]()
                sign_a(G, t)
                make_gate(G, t)
                if t == 0 and G > 0:
                    quantize_a(G - 1, second_tokens if G - 1 in in_halves else whole)
                if t == PACK - 1 and G in in_halves:
                    pack_a(G, first_tokens)
                    pack_a(G, second_tokens)
                    quantize_a(G, first_tokens)
                elif t == PACK - 1:
                    pack_a(G, whole)
                ahead = PACK * G + t + len(U_BANKS)
                if ahead < PACK * GROUPS:
                    encode(ahead)
                j = t if G - 1 in in_halves else t - 1
                if G > 0 and 0 <= j < LAST:
                    for h in range(HALVES):
                        decode_half(XAUX, j, h, [G - 1])
        gate_f(0, 1)
        quantize_a(GROUPS - 1, second_tokens)

        for h in range(HALVES):
            decode_half(XAUX, LAST, h, range(GROUPS - 1))
        pack_f(0, 0, nc.scalar.copy)
        pack_f(1, 0, nc.scalar.copy)
        for j in range(TILES):
            for h in range(HALVES):
                decode_half(XAUX, j, h, [GROUPS - 1])
                store_half(XAUX, j, h)

        f_steps = (
            ((quantize_f, 0, 0), (pack_f, 0, 1), (gate_f, 1, 1), (quantize_f, 0, 1), (pack_f, 1, 1), (quantize_f, 1, 0)),
            ((pack_f, 2, 0), (quantize_f, 1, 1), (gate_f, 2, 1), (quantize_f, 2, 0), (pack_f, 2, 1)),
            ((gate_f, 3, 1), (quantize_f, 2, 1), (pack_f, 3, 0), (pack_f, 3, 1), (quantize_f, 3, 0)),
            ((quantize_f, 3, 1),),
        )
        for j in range(TILES):
            for step, tile_index, pair in f_steps[j]:
                step(tile_index, pair)
            if j < LAST:
                for h in range(HALVES):
                    decode_half(XHAT, j, h, range(2))
                for h in range(HALVES):
                    decode_half(XHAT, j, h, range(2, GROUPS))
                    store_half(XHAT, j, h)

        decode_half(XHAT, LAST, 0, range(GROUPS))
        store_half(XHAT, LAST, 0)
        for q in range(BANK // P):
            d0, acc = BANK + P * q, bank[q][:, 0:P]
            for G in range(GROUPS):
                decode(XHAT, LAST, G, d0, acc)
            store(XHAT, LAST, d0, acc, nc.vector.tensor_copy if q % 2 == 0 else nc.scalar.copy)
